import numpy as np
import ml_dtypes


def mxq(x, axis, fmt="e4m3"):
    dtype, down = {"e4m3": (ml_dtypes.float8_e4m3fn, 7), "e5m2": (ml_dtypes.float8_e5m2, 14)}[fmt]
    v = np.moveaxis(np.asarray(x, np.float32).astype(ml_dtypes.bfloat16).astype(np.float64), axis, -1)
    blocks = v.reshape(v.shape[:-1] + (-1, 32))
    amax = np.abs(blocks).max(-1, keepdims=True)
    byte = np.maximum(np.where(amax > 0, np.frexp(amax)[1] - 1 + 127, 0) - down, 1)
    scale = np.exp2(byte - 127.0)
    codes = (blocks / scale).astype(np.float32).astype(dtype).astype(np.float64)
    return np.moveaxis((codes * scale).reshape(v.shape), -1, axis)


WIDE = False


def mx_kscale(k):
    if not WIDE:
        return np.ones(k)
    levels = np.array([10, -10, 5, -5, 0])
    if k % 512:
        return np.exp2(np.random.permutation(np.resize(levels, k // 32))).repeat(32)
    a = np.empty((k // 512, 16))
    for p in range(k // 512):
        a[p, :8] = np.random.permutation(np.resize(levels, 8))
        for g in range(8):
            far = levels[np.abs(levels - a[p, g]) >= 10]
            a[p, g + 8] = far[np.random.randint(len(far))]
    return np.exp2(a.ravel()).repeat(32)


BF16 = ml_dtypes.bfloat16


def bf(x):
    return np.asarray(x, np.float32).astype(BF16)


def f64(x):
    return np.asarray(x).astype(np.float64)

def planes(Y):
    n, m = Y.shape
    b = f64(bf(Y)).reshape(n // 32, 32, m)
    amax = np.abs(b).max(1)
    byte = np.clip(np.where(amax > 0, np.frexp(amax)[1] - 1 + 127 - 7, 1), 1, 254)
    codes = (b * np.exp2(127.0 - byte)[:, None, :]).reshape(n, m).astype(np.float32).astype(ml_dtypes.float8_e4m3fn).view(np.uint8)
    words = codes.reshape(n // 512, 128, 4, m).transpose(0, 1, 3, 2)
    return np.ascontiguousarray(words), np.ascontiguousarray(byte.astype(np.uint8).reshape(n // 512, 16, m))


N, K, T = 1024, 1024, 2


def stokes_mask(lam):
    return np.where(lam[None, :] > lam[:, None], 1.0, 0.0)


def surface_bounce(radiance, emitted, rho_t, conc_t):
    return rho_t[None, :] * radiance + conc_t[:, None] * emitted


def setup_inputs():
    s = mx_kscale(K)
    t = mx_kscale(K)
    c = 1.4 / np.sqrt(K)
    rho = np.random.uniform(0.3, 1.0, (T, K))
    rho[0] = rho[0] / s
    return {
        "l0": bf(np.random.standard_normal((N, K)) * s),
        "d1": bf(c * np.random.standard_normal((K, K)) / s[:, None]),
        "d2": bf(c * np.random.standard_normal((K, K)) / t[:, None]),
        "lam": bf(np.random.uniform(0.0, 1.0, K)),
        "rho": bf(rho),
        "conc": bf(np.random.uniform(0.5, 1.5, (T, N))),
        "a2": bf((1.0 + 0.1 * np.random.standard_normal(K)) * t),
    }


def core(l0, d1, d2, lam, rho, conc, a2):
    l0, d1, d2, lam, rho, conc, a2 = f64(l0), f64(d1), f64(d2), f64(lam), f64(rho), f64(conc), f64(a2)
    m = stokes_mask(lam)
    e1 = mxq(l0, 1, "e4m3") @ mxq(d1 * m, 0, "e4m3")
    l1 = surface_bounce(l0, e1, rho[0], conc[0])
    x2 = a2[None, :] * l1
    e2 = mxq(x2, 1, "e4m3") @ mxq(d2 * m, 0, "e4m3")
    return surface_bounce(l1, e2, rho[1], conc[1])


def reference(l0, d1, d2, lam, rho, conc, a2):
    R_out = core(l0, d1, d2, lam, rho, conc, a2)
    words, scales = planes(R_out.T)
    return R_out, words, scales

@@ -1,0 +1,368 @@
+from contextlib import ExitStack
+
+import concourse.mybir as mybir
+from concourse.masks import make_identity
+
+F32 = mybir.dt.float32
+BF16 = mybir.dt.bfloat16
+U32 = mybir.dt.uint32
+I32 = mybir.dt.int32
+U8 = mybir.dt.uint8
+FP8X4 = mybir.dt.float8_e4m3fn_x4
+ADD = mybir.AluOpType.add
+MULT = mybir.AluOpType.mult
+IS_GT = mybir.AluOpType.is_gt
+COPY = mybir.ActivationFunctionType.Copy
+
+P = 128
+N = 1024
+K = 1024
+G = 2
+BLK = 256
+NQ = N // BLK
+EB = 2
+CB = 3
+OB = 3
+FLOPS = 2 * 2 * N * K * K
+
+
+def tile_bispectralfluorescenttwobouncetransport_x1_kernel(
+    tc, l0, d1, d2, lam, rho, conc, a2, out_0, out_1, out_2
+):
+    nc = tc.nc
+    with ExitStack() as ctx:
+        sb = ctx.enter_context(tc.tile_pool(name="sb", bufs=1))
+        ps = ctx.enter_context(tc.psum_pool(name="ps", bufs=1))
+
+        def sbuf(shape, dtype, name, tag=None, bufs=1):
+            return sb.tile(shape, dtype, name=name, tag=tag or name, bufs=bufs, align_bytes=64)
+
+        def psum(shape, dtype, name, tag, bufs):
+            return ps.tile(shape, dtype, name=name, tag=tag, bufs=bufs)
+
+        vt = sbuf([P, 640], BF16, "vt")
+        nc.vector.memset(vt[:], 0.0)
+        nc.scalar.dma_start(out=vt[16:24, 512:640], in_=lam.rearrange("(r c) -> r c", c=P))
+        nc.scalar.dma_start(out=vt[0:2, 0:512], in_=lam.rearrange("(r c) -> r c", c=512))
+        nc.scalar.dma_start(out=vt[2:6, 0:512], in_=rho.rearrange("s (r c) -> (s r) c", c=512))
+        nc.scalar.dma_start(out=vt[6:8, 0:512], in_=a2.rearrange("(r c) -> r c", c=512))
+        nc.scalar.dma_start(out=vt[0:16, 512:640], in_=conc.rearrange("s (r c) -> (s r) c", c=P))
+
+        l0_sb = {}
+
+        def load_l0(i):
+            l0_sb[i] = sbuf([P, K], BF16, "l0_%d" % i)
+            nc.sync.dma_start(out=l0_sb[i][:], in_=l0[i * P : (i + 1) * P, :])
+
+        raw = {}
+
+        def load_d(which, src, g):
+            t = sbuf([P, 4, K], BF16, "raw_%d_%d" % (which, g))
+            v = src[g * 512 : (g + 1) * 512, :].rearrange("(p e) j -> p e j", e=4)
+            nc.sync.dma_start(out=t[:, 0:2, :], in_=v[:, 0:2, :])
+            nc.sync.dma_start(out=t[:, 2:4, :], in_=v[:, 2:4, :])
+            raw[which, g] = t
+
+        load_l0(0)
+        load_l0(1)
+        load_d(1, d1, 0)
+        load_d(1, d1, 1)
+        load_l0(2)
+        load_l0(3)
+        load_d(2, d2, 0)
+        load_d(2, d2, 1)
+        load_l0(4)
+        load_l0(5)
+        load_l0(6)
+        load_l0(7)
+
+        id_b = sbuf([P, P], BF16, "id_b")
+        make_identity(nc, id_b[:])
+        id_f = sbuf([P, P], F32, "id_f")
+        make_identity(nc, id_f[:])
+
+        vps = psum([P, 5, P], BF16, "vps", "ct", CB)
+        nc.tensor.transpose(vps[:, 4, :], vt[:, 512:640], id_b[:])
+        for e in range(4):
+            nc.tensor.transpose(vps[:, e, :], vt[:, e:512:4], id_b[:])
+        lamc = sbuf([P, 8], BF16, "lamc")
+        nc.vector.tensor_copy(out=lamc[:], in_=vps[:, 4, 16:24])
+        cols = sbuf([P, 5, 24], F32, "cols")
+        nc.vector.tensor_copy(out=cols[:], in_=vps[:, :, 0:24])
+        a2c = sbuf([P, 4, 2], F32, "a2c")
+        nc.vector.tensor_copy(out=a2c[:], in_=vps[:, 0:4, 6:8])
+        lps = psum([P, K], BF16, "lps", "ct", CB)
+        for c in range(8):
+            nc.tensor.transpose(lps[:, c * P : (c + 1) * P], lamc[:, c : c + 1].to_broadcast([P, P]), id_b[:])
+        lam_bc = sbuf([P, K], BF16, "lam_bc")
+        nc.scalar.copy(out=lam_bc[:], in_=lps[:])
+
+        def lam_col(g, e):
+            return cols[:, e, g : g + 1]
+
+        def rho_col(s, g, e):
+            r = 2 + 2 * s + g
+            return cols[:, e, r : r + 1]
+
+        def conc_col(s, i):
+            r = 8 * s + i
+            return cols[:, 4, r : r + 1]
+
+        mask = sbuf([P, G, 4, K], BF16, "mask")
+
+        def make_mask(g, h):
+            for e in range(4):
+                nc.vector.tensor_scalar(
+                    out=mask[:, g, e, h * 512 : (h + 1) * 512],
+                    in0=lam_bc[:, h * 512 : (h + 1) * 512],
+                    scalar1=lam_col(g, e),
+                    scalar2=None,
+                    op0=IS_GT,
+                )
+
+        d_codes = {}
+        d_scales = {}
+        for which in (1, 2):
+            d_codes[which] = sbuf([P, G, K], U32, "dc_%d" % which)
+            d_scales[which] = sbuf([P, G, K], U8, "ds_%d" % which)
+
+        def mask_mul(which, g, h):
+            t = raw[which, g][:, :, h * 512 : (h + 1) * 512]
+            nc.vector.tensor_tensor(out=t, in0=t, in1=mask[:, g, :, h * 512 : (h + 1) * 512], op=MULT)
+
+        def interleave_s(which, g, h):
+            grp = sbuf([P, 512, 4], BF16, "grp_%d_%d_%d" % (which, g, h), tag="grp", bufs=4)
+            src = raw[which, g][:, :, h * 512 : (h + 1) * 512]
+            for c0 in (0, 256):
+                nc.scalar.copy(
+                    out=grp[:, c0 : c0 + 256, :].rearrange("p (c i) t -> p c t i", i=4),
+                    in_=src[:, :, c0 : c0 + 256].rearrange("p t (c i) -> p c t i", i=4),
+                )
+            return grp
+
+        def interleave_v(which, g, h):
+            grp = sbuf([P, 512, 4], BF16, "grp_%d_%d_%d" % (which, g, h), tag="grp", bufs=4)
+            src = raw[which, g][:, :, h * 512 : (h + 1) * 512]
+            msk = mask[:, g, :, h * 512 : (h + 1) * 512]
+            nc.vector.tensor_tensor(
+                out=grp[:],
+                in0=src.rearrange("p t j -> p j t"),
+                in1=msk.rearrange("p t j -> p j t"),
+                op=MULT,
+            )
+            return grp
+
+        def quant_d(which, g, h, grp):
+            nc.vector.quantize_mx(
+                out=d_codes[which][:, g, h * 512 : (h + 1) * 512].bitcast(FP8X4),
+                scales=d_scales[which][:, g, h * 512 : (h + 1) * 512],
+                in_=grp[:].rearrange("p j t -> p (j t)"),
+            )
+
+        l0t = {}
+        l0_codes = {}
+        l0_scales = {}
+
+        def l0_turn(q):
+            t = sbuf([P, G, BLK, 2], F32, "l0t_%d" % q)
+            l0t[q] = t
+            for a in range(2):
+                words = l0_sb[2 * q + a][:].bitcast(F32)
+                bank = psum([P, G, 2, P], F32, "lb_%d_%d" % (q, a), "ob", OB)
+                for g in range(G):
+                    for u in range(2):
+                        nc.tensor.transpose(
+                            bank[:, g, u, :], words[:, 256 * g + u : 256 * (g + 1) : 2], id_f[:]
+                        )
+                nc.scalar.copy(
+                    out=t[:, :, a * P : (a + 1) * P, :], in_=bank[:].rearrange("p g u r -> p g r u")
+                )
+
+        def l0_quant(q):
+            l0_codes[q] = sbuf([P, G, BLK], U32, "l0c_%d" % q)
+            l0_scales[q] = sbuf([P, G, BLK], U8, "l0s_%d" % q)
+            nc.vector.quantize_mx(
+                out=l0_codes[q][:].rearrange("p g n -> p (g n)").bitcast(FP8X4),
+                scales=l0_scales[q][:].rearrange("p g n -> p (g n)"),
+                in_=l0t[q][:].bitcast(BF16).rearrange("p g n t -> p (g n t)"),
+            )
+
+        c_sb = {}
+
+        def product(stage, q, h):
+            xc, xs = (l0_codes[q], l0_scales[q]) if stage == 1 else (x2c[q], x2s[q])
+            for a in range(2):
+                bank = psum([P, 512], F32, "e_%d_%d_%d_%d" % (stage, q, a, h), "e", EB)
+                for g in range(G):
+                    nc.tensor.matmul_mx(
+                        out=bank[:],
+                        lhsT=xc[:, g, a * P : (a + 1) * P].bitcast(FP8X4),
+                        lhsT_scale=xs[:, g, a * P : (a + 1) * P],
+                        rhs=d_codes[stage][:, g, h * 512 : (h + 1) * 512].bitcast(FP8X4),
+                        rhs_scale=d_scales[stage][:, g, h * 512 : (h + 1) * 512],
+                        start=(g == 0),
+                        stop=(g == G - 1),
+                    )
+                c = sbuf([P, 4, P], F32, "c_%d_%d_%d_%d" % (stage, q, a, h), tag="c", bufs=6)
+                nc.scalar.activation(
+                    out=c[:],
+                    in_=bank[:].rearrange("n (m t) -> n t m", t=4),
+                    func=COPY,
+                    scale=conc_col(stage - 1, 2 * q + a),
+                )
+                c_sb[stage, q, h, a] = c
+
+        l1t = {}
+        x2c = {}
+        x2s = {}
+        x2 = {}
+        outt = {}
+        obf = {}
+        out_scales = sbuf([P, G, N], U8, "out_scales")
+
+        def turn(stage, q, h):
+            if h == 0:
+                if stage == 1:
+                    l1t[q] = sbuf([P, G, 4, BLK], F32, "l1t_%d" % q)
+                else:
+                    outt[q] = sbuf([P, G, 4, BLK], F32, "outt_%d" % q, tag="outt", bufs=2)
+            l0v = l0t[q][:].bitcast(BF16)
+            for tp in range(2):
+                bank = psum([P, 2, BLK], F32, "ct_%d_%d_%d_%d" % (stage, q, h, tp), "ct", CB)
+                for tt in range(2):
+                    for a in range(2):
+                        nc.tensor.transpose(
+                            bank[:, tt, a * P : (a + 1) * P], c_sb[stage, q, h, a][:, 2 * tp + tt, :], id_f[:]
+                        )
+                for tt in range(2):
+                    t = 2 * tp + tt
+                    nc.vector.scalar_tensor_tensor(
+                        out=l1t[q][:, h, t, :] if stage == 1 else outt[q][:, h, t, :],
+                        in0=l0v[:, h, :, t] if stage == 1 else l1t[q][:, h, t, :],
+                        scalar=rho_col(stage - 1, h, t),
+                        in1=bank[:, tt, :],
+                        op0=MULT,
+                        op1=ADD,
+                    )
+
+        def weigh(q, h):
+            x = sbuf([P, BLK, 4], BF16, "x2_%d_%d" % (q, h), tag="x2", bufs=4)
+            nc.vector.tensor_tensor(
+                out=x[:],
+                in0=l1t[q][:, h, :, :].rearrange("p t n -> p n t"),
+                in1=a2c[:, :, h : h + 1].rearrange("p t o -> p o t").to_broadcast([P, BLK, 4]),
+                op=MULT,
+            )
+            x2[q, h] = x
+
+        def weigh_quant(q, h):
+            if h == 0:
+                x2c[q] = sbuf([P, G, BLK], U32, "x2c_%d" % q)
+                x2s[q] = sbuf([P, G, BLK], U8, "x2s_%d" % q)
+            nc.vector.quantize_mx(
+                out=x2c[q][:, h, :].bitcast(FP8X4),
+                scales=x2s[q][:, h, :],
+                in_=x2[q, h][:].rearrange("p n t -> p (n t)"),
+            )
+
+        def round_out(q, h, eng):
+            o = sbuf([P, BLK, 4], BF16, "ob_%d_%d" % (q, h), tag="obf", bufs=4)
+            src = outt[q][:, h, :, :].rearrange("p t n -> p n t")
+            if eng == "G":
+                nc.gpsimd.tensor_scalar(out=o[:], in0=src, scalar1=1.0, scalar2=-0.0, op0=MULT, op1=ADD)
+            else:
+                nc.vector.tensor_copy(out=o[:], in_=src)
+            obf[q, h] = o
+
+        osb = {}
+
+        def back(q, h, engs="SS"):
+            for a in range(2):
+                if h == 0:
+                    osb[q, a] = sbuf([P, K], F32, "osb_%d_%d" % (q, a), tag="osb", bufs=3)
+                bank = psum([P, 4, P], F32, "bk_%d_%d_%d" % (q, a, h), "ob", OB)
+                for t in range(4):
+                    nc.tensor.transpose(bank[:, t, :], outt[q][:, h, t, a * P : (a + 1) * P], id_f[:])
+                dst = osb[q, a][:, h * 512 : (h + 1) * 512].rearrange("n (p t) -> n p t", t=4)
+                srcb = bank[:].rearrange("n t p -> n p t")
+                if engs[a] == "S":
+                    nc.scalar.copy(out=dst, in_=srcb)
+                else:
+                    nc.vector.tensor_copy(out=dst, in_=srcb)
+                if h == 1:
+                    i = 2 * q + a
+                    nc.sync.dma_start(out=out_0[i * P : (i + 1) * P, :], in_=osb[q, a][:])
+
+        def out_quant(q, h):
+            n0 = q * BLK
+            wc = sbuf([P, BLK], U32, "wc_%d_%d" % (q, h), tag="wc", bufs=4)
+            nc.vector.quantize_mx(
+                out=wc[:].bitcast(FP8X4),
+                scales=out_scales[:, h, n0 : n0 + BLK],
+                in_=obf[q, h][:].rearrange("p n t -> p (n t)"),
+            )
+            nc.sync.dma_start(
+                out=out_1[h, :, n0 : n0 + BLK, :].rearrange("p n t -> p (n t)").bitcast(I32),
+                in_=wc[:].bitcast(I32),
+            )
+
+        def store_scales(n0, n1):
+            for r in range(4):
+                nc.sync.dma_start(
+                    out=out_2[:, 4 * r : 4 * r + 4, n0:n1].rearrange("g r n -> r g n").bitcast(I32),
+                    in_=out_scales[32 * r : 32 * r + 4, :, n0:n1].bitcast(I32),
+                )
+
+        grp = {}
+        def prep(which, g, h):
+            mask_mul(which, g, h)
+            grp[which, g, h] = interleave_s(which, g, h)
+
+        l0_turn(0)
+        l0_quant(0)
+        for g, h in ((0, 0), (1, 0), (0, 1)):
+            make_mask(g, h)
+            prep(1, g, h)
+        make_mask(1, 1)
+        quant_d(1, 0, 0, grp[1, 0, 0])
+        grp[1, 1, 1] = interleave_v(1, 1, 1)
+        quant_d(1, 1, 0, grp[1, 1, 0])
+        product(1, 0, 0)
+        quant_d(1, 1, 1, grp[1, 1, 1])
+        quant_d(1, 0, 1, grp[1, 0, 1])
+        l0_turn(1)
+        l0_quant(1)
+        seq = [(1, 0, 0), (1, 0, 1), (1, 1, 0), (1, 1, 1), (2, 0, 0), (1, 2, 0), (2, 0, 1), (1, 2, 1),
+               (2, 1, 0), (1, 3, 0), (2, 1, 1), (1, 3, 1), (2, 2, 0), (2, 2, 1), (2, 3, 0), (2, 3, 1)]
+        d2q = [(0, 0), (1, 0), (0, 1), (1, 1)]
+        pend = []
+        for k, (s, q, h) in enumerate(seq):
+            if k < 4:
+                mask_mul(2, d2q[k][0], d2q[k][1])
+            if k + 1 < len(seq):
+                product(*seq[k + 1])
+            if k < 4:
+                grp[2, d2q[k][0], d2q[k][1]] = interleave_s(2, d2q[k][0], d2q[k][1])
+            turn(s, q, h)
+            if k in (1, 4):
+                l0_turn(2 if k == 1 else 3)
+            if k in (2, 5):
+                l0_quant(2 if k == 2 else 3)
+            if 1 <= k <= 4:
+                quant_d(2, d2q[k - 1][0], d2q[k - 1][1], grp[2, d2q[k - 1][0], d2q[k - 1][1]])
+            if s == 1:
+                weigh(q, h)
+            else:
+                round_out(q, h, "G")
+            if k >= 1:
+                s1, q1, h1 = seq[k - 1]
+                if s1 == 1:
+                    weigh_quant(q1, h1)
+                else:
+                    back(q1, h1)
+                    out_quant(q1, h1)
+                    if (q1, h1) == (1, 1):
+                        store_scales(0, 512)
+        back(3, 1, "SV")
+        out_quant(3, 1)
+        store_scales(512, 1024)

@@ -23,6 +23,7 @@ NQ = N // BLK
 EB = 2
 CB = 3
 OB = 3
+CFG = {'d1v': True, 'LA': 1, 'seq': [(1,0,0),(1,1,0),(1,0,1),(1,1,1),(1,2,0),(2,0,0),(1,2,1),(2,0,1),(1,3,0),(2,1,0),(1,3,1),(2,1,1),(2,2,0),(2,2,1),(2,3,0),(2,3,1)], 'd2k': 1, 'perm': 'mpitlndwqbo', 'l0': (1, 3), 'dq': 0, 'wl': 0, 'castG': 11, 'cE': 'S', 'pv': 16, 'ql': 1, 'ol': 1, 'bl': 1, 'sv': 12}
 FLOPS = 2 * 2 * N * K * K
 
 
@@ -40,13 +41,17 @@ def tile_bispectralfluorescenttwobouncetransport_x1_kernel(
         def psum(shape, dtype, name, tag, bufs):
             return ps.tile(shape, dtype, name=name, tag=tag, bufs=bufs)
 
-        vt = sbuf([P, 640], BF16, "vt")
-        nc.vector.memset(vt[:], 0.0)
-        nc.scalar.dma_start(out=vt[16:24, 512:640], in_=lam.rearrange("(r c) -> r c", c=P))
-        nc.scalar.dma_start(out=vt[0:2, 0:512], in_=lam.rearrange("(r c) -> r c", c=512))
-        nc.scalar.dma_start(out=vt[2:6, 0:512], in_=rho.rearrange("s (r c) -> (s r) c", c=512))
-        nc.scalar.dma_start(out=vt[6:8, 0:512], in_=a2.rearrange("(r c) -> r c", c=512))
-        nc.scalar.dma_start(out=vt[0:16, 512:640], in_=conc.rearrange("s (r c) -> (s r) c", c=P))
+        lam_row = sbuf([P, 8], BF16, "lam_row")
+        nc.scalar.dma_start(out=lam_row[:], in_=lam.rearrange("(p c) -> p c", c=8))
+        lamc = sbuf([P, G, 4], BF16, "lamc")
+        nc.scalar.dma_start(out=lamc[:], in_=lam.rearrange("(g p t) -> p g t", g=G, t=4))
+        rhoc = sbuf([P, 2 * G, 4], BF16, "rhoc")
+        nc.scalar.dma_start(out=rhoc[:], in_=rho.rearrange("s (g p t) -> p (s g) t", g=G, t=4))
+        a2c = sbuf([P, G, 4], BF16, "a2c")
+        nc.scalar.dma_start(out=a2c[:], in_=a2.rearrange("(g p t) -> p g t", g=G, t=4))
+        conc_rows = sbuf([P, P], BF16, "conc_rows")
+        nc.gpsimd.memset(conc_rows[:], 0.0)
+        nc.scalar.dma_start(out=conc_rows[0:16, :], in_=conc.rearrange("s (r c) -> (s r) c", c=P))
 
         l0_sb = {}
 
@@ -63,50 +68,40 @@ def tile_bispectralfluorescenttwobouncetransport_x1_kernel(
             nc.sync.dma_start(out=t[:, 2:4, :], in_=v[:, 2:4, :])
             raw[which, g] = t
 
+        load_d(1, d1, 0)
         load_l0(0)
         load_l0(1)
-        load_d(1, d1, 0)
         load_d(1, d1, 1)
         load_l0(2)
         load_l0(3)
         load_d(2, d2, 0)
         load_d(2, d2, 1)
-        load_l0(4)
-        load_l0(5)
-        load_l0(6)
-        load_l0(7)
+        for i in range(4, 8):
+            load_l0(i)
 
         id_b = sbuf([P, P], BF16, "id_b")
         make_identity(nc, id_b[:])
         id_f = sbuf([P, P], F32, "id_f")
         make_identity(nc, id_f[:])
 
-        vps = psum([P, 5, P], BF16, "vps", "ct", CB)
-        nc.tensor.transpose(vps[:, 4, :], vt[:, 512:640], id_b[:])
-        for e in range(4):
-            nc.tensor.transpose(vps[:, e, :], vt[:, e:512:4], id_b[:])
-        lamc = sbuf([P, 8], BF16, "lamc")
-        nc.vector.tensor_copy(out=lamc[:], in_=vps[:, 4, 16:24])
-        cols = sbuf([P, 5, 24], F32, "cols")
-        nc.vector.tensor_copy(out=cols[:], in_=vps[:, :, 0:24])
-        a2c = sbuf([P, 4, 2], F32, "a2c")
-        nc.vector.tensor_copy(out=a2c[:], in_=vps[:, 0:4, 6:8])
-        lps = psum([P, K], BF16, "lps", "ct", CB)
+        lps = psum([P, 8, P], BF16, "lps", "ct", CB)
         for c in range(8):
-            nc.tensor.transpose(lps[:, c * P : (c + 1) * P], lamc[:, c : c + 1].to_broadcast([P, P]), id_b[:])
+            nc.tensor.transpose(lps[:, c, :], lam_row[:, c : c + 1].to_broadcast([P, P]), id_b[:])
         lam_bc = sbuf([P, K], BF16, "lam_bc")
-        nc.scalar.copy(out=lam_bc[:], in_=lps[:])
+        nc.vector.tensor_copy(out=lam_bc[:].rearrange("m (p c) -> m p c", c=8), in_=lps[:].rearrange("m c p -> m p c"))
+        cps = psum([P, P], BF16, "cps", "ct", CB)
+        nc.tensor.transpose(cps[:], conc_rows[:], id_b[:])
+        concc = sbuf([P, 16], F32, "concc")
+        nc.scalar.copy(out=concc[:], in_=cps[:, 0:16])
 
-        def lam_col(g, e):
-            return cols[:, e, g : g + 1]
+        def lam_col(g, t):
+            return lamc[:, g, t : t + 1]
 
-        def rho_col(s, g, e):
-            r = 2 + 2 * s + g
-            return cols[:, e, r : r + 1]
+        def rho_col(s, g, t):
+            return rhoc[:, 2 * s + g, t : t + 1]
 
         def conc_col(s, i):
-            r = 8 * s + i
-            return cols[:, 4, r : r + 1]
+            return concc[:, 8 * s + i : 8 * s + i + 1]
 
         mask = sbuf([P, G, 4, K], BF16, "mask")
 
@@ -189,7 +184,7 @@ def tile_bispectralfluorescenttwobouncetransport_x1_kernel(
 
         c_sb = {}
 
-        def product(stage, q, h):
+        def product(stage, q, h, engs="SS"):
             xc, xs = (l0_codes[q], l0_scales[q]) if stage == 1 else (x2c[q], x2s[q])
             for a in range(2):
                 bank = psum([P, 512], F32, "e_%d_%d_%d_%d" % (stage, q, a, h), "e", EB)
@@ -204,12 +199,12 @@ def tile_bispectralfluorescenttwobouncetransport_x1_kernel(
                         stop=(g == G - 1),
                     )
                 c = sbuf([P, 4, P], F32, "c_%d_%d_%d_%d" % (stage, q, a, h), tag="c", bufs=6)
-                nc.scalar.activation(
-                    out=c[:],
-                    in_=bank[:].rearrange("n (m t) -> n t m", t=4),
-                    func=COPY,
-                    scale=conc_col(stage - 1, 2 * q + a),
-                )
+                src = bank[:].rearrange("n (m t) -> n t m", t=4)
+                scale = conc_col(stage - 1, 2 * q + a)
+                if engs[a] == "S":
+                    nc.scalar.activation(out=c[:], in_=src, func=COPY, scale=scale)
+                else:
+                    nc.vector.tensor_scalar(out=c[:], in0=src, scalar1=scale, scalar2=None, op0=MULT)
                 c_sb[stage, q, h, a] = c
 
         l1t = {}
@@ -250,7 +245,7 @@ def tile_bispectralfluorescenttwobouncetransport_x1_kernel(
             nc.vector.tensor_tensor(
                 out=x[:],
                 in0=l1t[q][:, h, :, :].rearrange("p t n -> p n t"),
-                in1=a2c[:, :, h : h + 1].rearrange("p t o -> p o t").to_broadcast([P, BLK, 4]),
+                in1=a2c[:, h : h + 1, :].to_broadcast([P, BLK, 4]),
                 op=MULT,
             )
             x2[q, h] = x
@@ -270,6 +265,8 @@ def tile_bispectralfluorescenttwobouncetransport_x1_kernel(
             src = outt[q][:, h, :, :].rearrange("p t n -> p n t")
             if eng == "G":
                 nc.gpsimd.tensor_scalar(out=o[:], in0=src, scalar1=1.0, scalar2=-0.0, op0=MULT, op1=ADD)
+            elif eng == "S":
+                nc.scalar.copy(out=o[:], in_=src)
             else:
                 nc.vector.tensor_copy(out=o[:], in_=src)
             obf[q, h] = o
@@ -289,8 +286,13 @@ def tile_bispectralfluorescenttwobouncetransport_x1_kernel(
                     nc.scalar.copy(out=dst, in_=srcb)
                 else:
                     nc.vector.tensor_copy(out=dst, in_=srcb)
-                if h == 1:
-                    i = 2 * q + a
+                i = 2 * q + a
+                if q == NQ - 1:
+                    nc.sync.dma_start(
+                        out=out_0[i * P : (i + 1) * P, h * 512 : (h + 1) * 512],
+                        in_=osb[q, a][:, h * 512 : (h + 1) * 512],
+                    )
+                elif h == 1:
                     nc.sync.dma_start(out=out_0[i * P : (i + 1) * P, :], in_=osb[q, a][:])
 
         def out_quant(q, h):
@@ -314,55 +316,82 @@ def tile_bispectralfluorescenttwobouncetransport_x1_kernel(
                 )
 
         grp = {}
+
         def prep(which, g, h):
             mask_mul(which, g, h)
             grp[which, g, h] = interleave_s(which, g, h)
 
+        def qd(which, g, h):
+            quant_d(which, g, h, grp[which, g, h])
+
         l0_turn(0)
+        make_mask(0, 0)
+        make_mask(1, 0)
+        prep(1, 0, 0)
+        make_mask(0, 1)
+        prep(1, 1, 0)
         l0_quant(0)
-        for g, h in ((0, 0), (1, 0), (0, 1)):
-            make_mask(g, h)
-            prep(1, g, h)
-        make_mask(1, 1)
-        quant_d(1, 0, 0, grp[1, 0, 0])
-        grp[1, 1, 1] = interleave_v(1, 1, 1)
-        quant_d(1, 1, 0, grp[1, 1, 0])
-        product(1, 0, 0)
-        quant_d(1, 1, 1, grp[1, 1, 1])
-        quant_d(1, 0, 1, grp[1, 0, 1])
         l0_turn(1)
+        make_mask(1, 1)
+        prep(1, 0, 1)
+        qd(1, 0, 0)
+        if CFG["d1v"]:
+            grp[1, 1, 1] = interleave_v(1, 1, 1)
+        else:
+            mask_mul(1, 1, 1)
         l0_quant(1)
-        seq = [(1, 0, 0), (1, 0, 1), (1, 1, 0), (1, 1, 1), (2, 0, 0), (1, 2, 0), (2, 0, 1), (1, 2, 1),
-               (2, 1, 0), (1, 3, 0), (2, 1, 1), (1, 3, 1), (2, 2, 0), (2, 2, 1), (2, 3, 0), (2, 3, 1)]
+        qd(1, 1, 0)
+        seq = CFG["seq"]
+        for k in range(CFG["LA"]):
+            product(*seq[k])
+        if not CFG["d1v"]:
+            grp[1, 1, 1] = interleave_s(1, 1, 1)
+        qd(1, 0, 1)
         d2q = [(0, 0), (1, 0), (0, 1), (1, 1)]
-        pend = []
-        for k, (s, q, h) in enumerate(seq):
-            if k < 4:
-                mask_mul(2, d2q[k][0], d2q[k][1])
-            if k + 1 < len(seq):
-                product(*seq[k + 1])
-            if k < 4:
-                grp[2, d2q[k][0], d2q[k][1]] = interleave_s(2, d2q[k][0], d2q[k][1])
-            turn(s, q, h)
-            if k in (1, 4):
-                l0_turn(2 if k == 1 else 3)
-            if k in (2, 5):
-                l0_quant(2 if k == 2 else 3)
-            if 1 <= k <= 4:
-                quant_d(2, d2q[k - 1][0], d2q[k - 1][1], grp[2, d2q[k - 1][0], d2q[k - 1][1]])
-            if s == 1:
-                weigh(q, h)
-            else:
-                round_out(q, h, "G")
-            if k >= 1:
-                s1, q1, h1 = seq[k - 1]
-                if s1 == 1:
-                    weigh_quant(q1, h1)
-                else:
-                    back(q1, h1)
-                    out_quant(q1, h1)
-                    if (q1, h1) == (1, 1):
-                        store_scales(0, 512)
-        back(3, 1, "SV")
-        out_quant(3, 1)
+        if CFG["d2k"] == 0:
+            prep(2, 0, 0)
+        qd(1, 1, 1)
+        o = 1 if CFG["d2k"] == 0 else 0
+        for k in range(len(seq) + 2):
+            for c in CFG["perm"]:
+                if c == "m" and 0 <= k + o < 4 and not (k + o == 0 and o):
+                    mask_mul(2, *d2q[k + o])
+                if c == "p" and k + CFG["LA"] < len(seq):
+                    product(*seq[k + CFG["LA"]], "SS" if k + CFG["LA"] < CFG["pv"] else "SV")
+                if c == "i" and 0 <= k + o < 4 and not (k + o == 0 and o):
+                    grp[(2,) + d2q[k + o]] = interleave_s(2, *d2q[k + o])
+                if c == "t" and k < len(seq):
+                    turn(*seq[k])
+                if c == "l":
+                    for j in (0, 1):
+                        if k == CFG["l0"][j]:
+                            l0_turn(2 + j)
+                if c == "n":
+                    for j in (0, 1):
+                        if k == CFG["l0"][j] + 1:
+                            l0_quant(2 + j)
+                if c == "d" and 0 <= k + o - CFG["dq"] < 4:
+                    qd(2, *d2q[k + o - CFG["dq"]])
+                if c == "w":
+                    kk = k - CFG["wl"]
+                    if 0 <= kk < len(seq):
+                        s, q, h = seq[kk]
+                        if s == 1:
+                            weigh(q, h)
+                        else:
+                            round_out(q, h, CFG["cE"] if kk < CFG["castG"] else "V")
+                if c == "q":
+                    kk = k - CFG["ql"]
+                    if 0 <= kk < len(seq) and seq[kk][0] == 1:
+                        weigh_quant(*seq[kk][1:])
+                if c == "o":
+                    kk = k - CFG["ol"]
+                    if 0 <= kk < len(seq) and seq[kk][0] == 2:
+                        out_quant(*seq[kk][1:])
+                        if seq[kk] == (2, 1, 1):
+                            store_scales(0, 512)
+                if c == "b":
+                    kk = k - CFG["bl"]
+                    if 0 <= kk < len(seq) and seq[kk][0] == 2:
+                        back(*seq[kk][1:], "SS" if kk < CFG["sv"] else "SV")
         store_scales(512, 1024)

from contextlib import ExitStack

import concourse.mybir as mybir
from concourse.masks import make_identity

F32 = mybir.dt.float32
BF16 = mybir.dt.bfloat16
U32 = mybir.dt.uint32
I32 = mybir.dt.int32
U8 = mybir.dt.uint8
FP8X4 = mybir.dt.float8_e4m3fn_x4
ADD = mybir.AluOpType.add
MULT = mybir.AluOpType.mult
IS_GT = mybir.AluOpType.is_gt
COPY = mybir.ActivationFunctionType.Copy

P = 128
N = 1024
K = 1024
G = 2
BLK = 256
NQ = N // BLK
EB = 2
CB = 3
OB = 3
CFG = {'d1v': True, 'LA': 1, 'seq': [(1,0,0),(1,1,0),(1,0,1),(1,1,1),(1,2,0),(2,0,0),(1,2,1),(2,0,1),(1,3,0),(2,1,0),(1,3,1),(2,1,1),(2,2,0),(2,2,1),(2,3,0),(2,3,1)], 'd2k': 1, 'perm': 'mpitlndwqbo', 'l0': (1, 3), 'dq': 0, 'wl': 0, 'castG': 11, 'cE': 'S', 'pv': 16, 'ql': 1, 'ol': 1, 'bl': 1, 'sv': 12}
FLOPS = 2 * 2 * N * K * K


def tile_bispectralfluorescenttwobouncetransport_x1_kernel(
    tc, l0, d1, d2, lam, rho, conc, a2, out_0, out_1, out_2
):
    nc = tc.nc
    with ExitStack() as ctx:
        sb = ctx.enter_context(tc.tile_pool(name="sb", bufs=1))
        ps = ctx.enter_context(tc.psum_pool(name="ps", bufs=1))

        def sbuf(shape, dtype, name, tag=None, bufs=1):
            return sb.tile(shape, dtype, name=name, tag=tag or name, bufs=bufs, align_bytes=64)

        def psum(shape, dtype, name, tag, bufs):
            return ps.tile(shape, dtype, name=name, tag=tag, bufs=bufs)

        lam_row = sbuf([P, 8], BF16, "lam_row")
        nc.scalar.dma_start(out=lam_row[:], in_=lam.rearrange("(p c) -> p c", c=8))
        lamc = sbuf([P, G, 4], BF16, "lamc")
        nc.scalar.dma_start(out=lamc[:], in_=lam.rearrange("(g p t) -> p g t", g=G, t=4))
        rhoc = sbuf([P, 2 * G, 4], BF16, "rhoc")
        nc.scalar.dma_start(out=rhoc[:], in_=rho.rearrange("s (g p t) -> p (s g) t", g=G, t=4))
        a2c = sbuf([P, G, 4], BF16, "a2c")
        nc.scalar.dma_start(out=a2c[:], in_=a2.rearrange("(g p t) -> p g t", g=G, t=4))
        conc_rows = sbuf([P, P], BF16, "conc_rows")
        nc.gpsimd.memset(conc_rows[:], 0.0)
        nc.scalar.dma_start(out=conc_rows[0:16, :], in_=conc.rearrange("s (r c) -> (s r) c", c=P))

        l0_sb = {}

        def load_l0(i):
            l0_sb[i] = sbuf([P, K], BF16, "l0_%d" % i)
            nc.sync.dma_start(out=l0_sb[i][:], in_=l0[i * P : (i + 1) * P, :])

        raw = {}

        def load_d(which, src, g):
            t = sbuf([P, 4, K], BF16, "raw_%d_%d" % (which, g))
            v = src[g * 512 : (g + 1) * 512, :].rearrange("(p e) j -> p e j", e=4)
            nc.sync.dma_start(out=t[:, 0:2, :], in_=v[:, 0:2, :])
            nc.sync.dma_start(out=t[:, 2:4, :], in_=v[:, 2:4, :])
            raw[which, g] = t

        load_d(1, d1, 0)
        load_l0(0)
        load_l0(1)
        load_d(1, d1, 1)
        load_l0(2)
        load_l0(3)
        load_d(2, d2, 0)
        load_d(2, d2, 1)
        for i in range(4, 8):
            load_l0(i)

        id_b = sbuf([P, P], BF16, "id_b")
        make_identity(nc, id_b[:])
        id_f = sbuf([P, P], F32, "id_f")
        make_identity(nc, id_f[:])

        lps = psum([P, 8, P], BF16, "lps", "ct", CB)
        for c in range(8):
            nc.tensor.transpose(lps[:, c, :], lam_row[:, c : c + 1].to_broadcast([P, P]), id_b[:])
        lam_bc = sbuf([P, K], BF16, "lam_bc")
        nc.vector.tensor_copy(out=lam_bc[:].rearrange("m (p c) -> m p c", c=8), in_=lps[:].rearrange("m c p -> m p c"))
        cps = psum([P, P], BF16, "cps", "ct", CB)
        nc.tensor.transpose(cps[:], conc_rows[:], id_b[:])
        concc = sbuf([P, 16], F32, "concc")
        nc.scalar.copy(out=concc[:], in_=cps[:, 0:16])

        def lam_col(g, t):
            return lamc[:, g, t : t + 1]

        def rho_col(s, g, t):
            return rhoc[:, 2 * s + g, t : t + 1]

        def conc_col(s, i):
            return concc[:, 8 * s + i : 8 * s + i + 1]

        mask = sbuf([P, G, 4, K], BF16, "mask")

        def make_mask(g, h):
            for e in range(4):
                nc.vector.tensor_scalar(
                    out=mask[:, g, e, h * 512 : (h + 1) * 512],
                    in0=lam_bc[:, h * 512 : (h + 1) * 512],
                    scalar1=lam_col(g, e),
                    scalar2=None,
                    op0=IS_GT,
                )

        d_codes = {}
        d_scales = {}
        for which in (1, 2):
            d_codes[which] = sbuf([P, G, K], U32, "dc_%d" % which)
            d_scales[which] = sbuf([P, G, K], U8, "ds_%d" % which)

        def mask_mul(which, g, h):
            t = raw[which, g][:, :, h * 512 : (h + 1) * 512]
            nc.vector.tensor_tensor(out=t, in0=t, in1=mask[:, g, :, h * 512 : (h + 1) * 512], op=MULT)

        def interleave_s(which, g, h):
            grp = sbuf([P, 512, 4], BF16, "grp_%d_%d_%d" % (which, g, h), tag="grp", bufs=4)
            src = raw[which, g][:, :, h * 512 : (h + 1) * 512]
            for c0 in (0, 256):
                nc.scalar.copy(
                    out=grp[:, c0 : c0 + 256, :].rearrange("p (c i) t -> p c t i", i=4),
                    in_=src[:, :, c0 : c0 + 256].rearrange("p t (c i) -> p c t i", i=4),
                )
            return grp

        def interleave_v(which, g, h):
            grp = sbuf([P, 512, 4], BF16, "grp_%d_%d_%d" % (which, g, h), tag="grp", bufs=4)
            src = raw[which, g][:, :, h * 512 : (h + 1) * 512]
            msk = mask[:, g, :, h * 512 : (h + 1) * 512]
            nc.vector.tensor_tensor(
                out=grp[:],
                in0=src.rearrange("p t j -> p j t"),
                in1=msk.rearrange("p t j -> p j t"),
                op=MULT,
            )
            return grp

        def quant_d(which, g, h, grp):
            nc.vector.quantize_mx(
                out=d_codes[which][:, g, h * 512 : (h + 1) * 512].bitcast(FP8X4),
                scales=d_scales[which][:, g, h * 512 : (h + 1) * 512],
                in_=grp[:].rearrange("p j t -> p (j t)"),
            )

        l0t = {}
        l0_codes = {}
        l0_scales = {}

        def l0_turn(q):
            t = sbuf([P, G, BLK, 2], F32, "l0t_%d" % q)
            l0t[q] = t
            for a in range(2):
                words = l0_sb[2 * q + a][:].bitcast(F32)
                bank = psum([P, G, 2, P], F32, "lb_%d_%d" % (q, a), "ob", OB)
                for g in range(G):
                    for u in range(2):
                        nc.tensor.transpose(
                            bank[:, g, u, :], words[:, 256 * g + u : 256 * (g + 1) : 2], id_f[:]
                        )
                nc.scalar.copy(
                    out=t[:, :, a * P : (a + 1) * P, :], in_=bank[:].rearrange("p g u r -> p g r u")
                )

        def l0_quant(q):
            l0_codes[q] = sbuf([P, G, BLK], U32, "l0c_%d" % q)
            l0_scales[q] = sbuf([P, G, BLK], U8, "l0s_%d" % q)
            nc.vector.quantize_mx(
                out=l0_codes[q][:].rearrange("p g n -> p (g n)").bitcast(FP8X4),
                scales=l0_scales[q][:].rearrange("p g n -> p (g n)"),
                in_=l0t[q][:].bitcast(BF16).rearrange("p g n t -> p (g n t)"),
            )

        c_sb = {}

        def product(stage, q, h, engs="SS"):
            xc, xs = (l0_codes[q], l0_scales[q]) if stage == 1 else (x2c[q], x2s[q])
            for a in range(2):
                bank = psum([P, 512], F32, "e_%d_%d_%d_%d" % (stage, q, a, h), "e", EB)
                for g in range(G):
                    nc.tensor.matmul_mx(
                        out=bank[:],
                        lhsT=xc[:, g, a * P : (a + 1) * P].bitcast(FP8X4),
                        lhsT_scale=xs[:, g, a * P : (a + 1) * P],
                        rhs=d_codes[stage][:, g, h * 512 : (h + 1) * 512].bitcast(FP8X4),
                        rhs_scale=d_scales[stage][:, g, h * 512 : (h + 1) * 512],
                        start=(g == 0),
                        stop=(g == G - 1),
                    )
                c = sbuf([P, 4, P], F32, "c_%d_%d_%d_%d" % (stage, q, a, h), tag="c", bufs=6)
                src = bank[:].rearrange("n (m t) -> n t m", t=4)
                scale = conc_col(stage - 1, 2 * q + a)
                if engs[a] == "S":
                    nc.scalar.activation(out=c[:], in_=src, func=COPY, scale=scale)
                else:
                    nc.vector.tensor_scalar(out=c[:], in0=src, scalar1=scale, scalar2=None, op0=MULT)
                c_sb[stage, q, h, a] = c

        l1t = {}
        x2c = {}
        x2s = {}
        x2 = {}
        outt = {}
        obf = {}
        out_scales = sbuf([P, G, N], U8, "out_scales")

        def turn(stage, q, h):
            if h == 0:
                if stage == 1:
                    l1t[q] = sbuf([P, G, 4, BLK], F32, "l1t_%d" % q)
                else:
                    outt[q] = sbuf([P, G, 4, BLK], F32, "outt_%d" % q, tag="outt", bufs=2)
            l0v = l0t[q][:].bitcast(BF16)
            for tp in range(2):
                bank = psum([P, 2, BLK], F32, "ct_%d_%d_%d_%d" % (stage, q, h, tp), "ct", CB)
                for tt in range(2):
                    for a in range(2):
                        nc.tensor.transpose(
                            bank[:, tt, a * P : (a + 1) * P], c_sb[stage, q, h, a][:, 2 * tp + tt, :], id_f[:]
                        )
                for tt in range(2):
                    t = 2 * tp + tt
                    nc.vector.scalar_tensor_tensor(
                        out=l1t[q][:, h, t, :] if stage == 1 else outt[q][:, h, t, :],
                        in0=l0v[:, h, :, t] if stage == 1 else l1t[q][:, h, t, :],
                        scalar=rho_col(stage - 1, h, t),
                        in1=bank[:, tt, :],
                        op0=MULT,
                        op1=ADD,
                    )

        def weigh(q, h):
            x = sbuf([P, BLK, 4], BF16, "x2_%d_%d" % (q, h), tag="x2", bufs=4)
            nc.vector.tensor_tensor(
                out=x[:],
                in0=l1t[q][:, h, :, :].rearrange("p t n -> p n t"),
                in1=a2c[:, h : h + 1, :].to_broadcast([P, BLK, 4]),
                op=MULT,
            )
            x2[q, h] = x

        def weigh_quant(q, h):
            if h == 0:
                x2c[q] = sbuf([P, G, BLK], U32, "x2c_%d" % q)
                x2s[q] = sbuf([P, G, BLK], U8, "x2s_%d" % q)
            nc.vector.quantize_mx(
                out=x2c[q][:, h, :].bitcast(FP8X4),
                scales=x2s[q][:, h, :],
                in_=x2[q, h][:].rearrange("p n t -> p (n t)"),
            )

        def round_out(q, h, eng):
            o = sbuf([P, BLK, 4], BF16, "ob_%d_%d" % (q, h), tag="obf", bufs=4)
            src = outt[q][:, h, :, :].rearrange("p t n -> p n t")
            if eng == "G":
                nc.gpsimd.tensor_scalar(out=o[:], in0=src, scalar1=1.0, scalar2=-0.0, op0=MULT, op1=ADD)
            elif eng == "S":
                nc.scalar.copy(out=o[:], in_=src)
            else:
                nc.vector.tensor_copy(out=o[:], in_=src)
            obf[q, h] = o

        osb = {}

        def back(q, h, engs="SS"):
            for a in range(2):
                if h == 0:
                    osb[q, a] = sbuf([P, K], F32, "osb_%d_%d" % (q, a), tag="osb", bufs=3)
                bank = psum([P, 4, P], F32, "bk_%d_%d_%d" % (q, a, h), "ob", OB)
                for t in range(4):
                    nc.tensor.transpose(bank[:, t, :], outt[q][:, h, t, a * P : (a + 1) * P], id_f[:])
                dst = osb[q, a][:, h * 512 : (h + 1) * 512].rearrange("n (p t) -> n p t", t=4)
                srcb = bank[:].rearrange("n t p -> n p t")
                if engs[a] == "S":
                    nc.scalar.copy(out=dst, in_=srcb)
                else:
                    nc.vector.tensor_copy(out=dst, in_=srcb)
                i = 2 * q + a
                if q == NQ - 1:
                    nc.sync.dma_start(
                        out=out_0[i * P : (i + 1) * P, h * 512 : (h + 1) * 512],
                        in_=osb[q, a][:, h * 512 : (h + 1) * 512],
                    )
                elif h == 1:
                    nc.sync.dma_start(out=out_0[i * P : (i + 1) * P, :], in_=osb[q, a][:])

        def out_quant(q, h):
            n0 = q * BLK
            wc = sbuf([P, BLK], U32, "wc_%d_%d" % (q, h), tag="wc", bufs=4)
            nc.vector.quantize_mx(
                out=wc[:].bitcast(FP8X4),
                scales=out_scales[:, h, n0 : n0 + BLK],
                in_=obf[q, h][:].rearrange("p n t -> p (n t)"),
            )
            nc.sync.dma_start(
                out=out_1[h, :, n0 : n0 + BLK, :].rearrange("p n t -> p (n t)").bitcast(I32),
                in_=wc[:].bitcast(I32),
            )

        def store_scales(n0, n1):
            for r in range(4):
                nc.sync.dma_start(
                    out=out_2[:, 4 * r : 4 * r + 4, n0:n1].rearrange("g r n -> r g n").bitcast(I32),
                    in_=out_scales[32 * r : 32 * r + 4, :, n0:n1].bitcast(I32),
                )

        grp = {}

        def prep(which, g, h):
            mask_mul(which, g, h)
            grp[which, g, h] = interleave_s(which, g, h)

        def qd(which, g, h):
            quant_d(which, g, h, grp[which, g, h])

        l0_turn(0)
        make_mask(0, 0)
        make_mask(1, 0)
        prep(1, 0, 0)
        make_mask(0, 1)
        prep(1, 1, 0)
        l0_quant(0)
        l0_turn(1)
        make_mask(1, 1)
        prep(1, 0, 1)
        qd(1, 0, 0)
        if CFG["d1v"]:
            grp[1, 1, 1] = interleave_v(1, 1, 1)
        else:
            mask_mul(1, 1, 1)
        l0_quant(1)
        qd(1, 1, 0)
        seq = CFG["seq"]
        for k in range(CFG["LA"]):
            product(*seq[k])
        if not CFG["d1v"]:
            grp[1, 1, 1] = interleave_s(1, 1, 1)
        qd(1, 0, 1)
        d2q = [(0, 0), (1, 0), (0, 1), (1, 1)]
        if CFG["d2k"] == 0:
            prep(2, 0, 0)
        qd(1, 1, 1)
        o = 1 if CFG["d2k"] == 0 else 0
        for k in range(len(seq) + 2):
            for c in CFG["perm"]:
                if c == "m" and 0 <= k + o < 4 and not (k + o == 0 and o):
                    mask_mul(2, *d2q[k + o])
                if c == "p" and k + CFG["LA"] < len(seq):
                    product(*seq[k + CFG["LA"]], "SS" if k + CFG["LA"] < CFG["pv"] else "SV")
                if c == "i" and 0 <= k + o < 4 and not (k + o == 0 and o):
                    grp[(2,) + d2q[k + o]] = interleave_s(2, *d2q[k + o])
                if c == "t" and k < len(seq):
                    turn(*seq[k])
                if c == "l":
                    for j in (0, 1):
                        if k == CFG["l0"][j]:
                            l0_turn(2 + j)
                if c == "n":
                    for j in (0, 1):
                        if k == CFG["l0"][j] + 1:
                            l0_quant(2 + j)
                if c == "d" and 0 <= k + o - CFG["dq"] < 4:
                    qd(2, *d2q[k + o - CFG["dq"]])
                if c == "w":
                    kk = k - CFG["wl"]
                    if 0 <= kk < len(seq):
                        s, q, h = seq[kk]
                        if s == 1:
                            weigh(q, h)
                        else:
                            round_out(q, h, CFG["cE"] if kk < CFG["castG"] else "V")
                if c == "q":
                    kk = k - CFG["ql"]
                    if 0 <= kk < len(seq) and seq[kk][0] == 1:
                        weigh_quant(*seq[kk][1:])
                if c == "o":
                    kk = k - CFG["ol"]
                    if 0 <= kk < len(seq) and seq[kk][0] == 2:
                        out_quant(*seq[kk][1:])
                        if seq[kk] == (2, 1, 1):
                            store_scales(0, 512)
                if c == "b":
                    kk = k - CFG["bl"]
                    if 0 <= kk < len(seq) and seq[kk][0] == 2:
                        back(*seq[kk][1:], "SS" if kk < CFG["sv"] else "SV")
        store_scales(512, 1024)
